import numpy as np
import ml_dtypes


def mxq(x, axis, fmt="e4m3"):
    dtype, down = {"e4m3": (ml_dtypes.float8_e4m3fn, 7), "e5m2": (ml_dtypes.float8_e5m2, 14)}[fmt]
    v = np.moveaxis(np.asarray(x, np.float32).astype(ml_dtypes.bfloat16).astype(np.float64), axis, -1)
    blocks = v.reshape(v.shape[:-1] + (-1, 32))
    amax = np.abs(blocks).max(-1, keepdims=True)
    byte = np.maximum(np.where(amax > 0, np.frexp(amax)[1] - 1 + 127, 0) - down, 1)
    scale = np.exp2(byte - 127.0)
    codes = (blocks / scale).astype(np.float32).astype(dtype).astype(np.float64)
    return np.moveaxis((codes * scale).reshape(v.shape), -1, axis)


WIDE = False


def mx_kscale(k):
    if not WIDE:
        return np.ones(k)
    levels = np.array([10, -10, 5, -5, 0])
    if k % 512:
        return np.exp2(np.random.permutation(np.resize(levels, k // 32))).repeat(32)
    a = np.empty((k // 512, 16))
    for p in range(k // 512):
        a[p, :8] = np.random.permutation(np.resize(levels, 8))
        for g in range(8):
            far = levels[np.abs(levels - a[p, g]) >= 10]
            a[p, g + 8] = far[np.random.randint(len(far))]
    return np.exp2(a.ravel()).repeat(32)


BF16 = ml_dtypes.bfloat16


def bf(x):
    return np.asarray(x, np.float32).astype(BF16)


def f64(x):
    return np.asarray(x).astype(np.float64)


E2M1 = np.array([0.0, 0.5, 1.0, 1.5, 2.0, 3.0, 4.0, 6.0, -0.0, -0.5, -1.0, -1.5, -2.0, -3.0, -4.0, -6.0])


def pack_weight(w, fmt):
    k, n = w.shape
    w = f64(bf(w)).reshape(k // 32, 32, n)
    amax = np.abs(w).max(1)
    if fmt == "e4m3":
        byte = np.frexp(amax)[1] - 1 + 127 - 7
    else:
        mant, ex = np.frexp(amax / 6.0)
        byte = np.where(mant > 0.5, ex, ex - 1) + 127
    byte = np.clip(np.where(amax > 0, byte, 1), 1, 254)
    scaled = (w * np.exp2(127.0 - byte)[:, None, :]).reshape(k, n).astype(np.float32)
    by_word = np.ascontiguousarray(scaled.reshape(k // 512, 128, 4, n).transpose(0, 1, 3, 2))
    if fmt == "e4m3":
        words = by_word.astype(ml_dtypes.float8_e4m3fn).view(np.uint8)
    else:
        c = by_word.astype(ml_dtypes.float4_e2m1fn).view(np.uint8) & 0xF
        words = c[..., 0::2] | (c[..., 1::2] << 4)
    return np.ascontiguousarray(words), np.ascontiguousarray(byte.astype(np.uint8).reshape(k // 512, 16, n))


def unpack_weight(words, scales, fmt):
    g, p, n, _ = words.shape
    if fmt == "e4m3":
        vals = np.ascontiguousarray(words).view(ml_dtypes.float8_e4m3fn).astype(np.float64)
    else:
        nib = np.empty((g, p, n, 4), np.uint8)
        nib[..., 0::2] = words & 0xF
        nib[..., 1::2] = words >> 4
        vals = E2M1[nib]
    vals = vals * np.repeat(np.exp2(scales.astype(np.float64) - 127.0), 8, axis=1)[..., None]
    return vals.transpose(0, 1, 3, 2).reshape(g * 512, n)
def pack4(w):
    words, scales = pack_weight(w, "e2m1")
    return words.reshape(words.shape[0], 128, -1), scales


def unpack4(words, scales):
    return unpack_weight(words.reshape(words.shape[0], 128, -1, 2), scales, "e2m1")


D = 1024


def setup_inputs():
    s, t = mx_kscale(D), mx_kscale(D)
    w = np.exp(0.5 * np.random.standard_normal((D, D)))
    w = (w - w.mean()) / w.std() / D ** 0.25
    left_words, left_scales = pack4(w.T * s[:, None])
    right_words, right_scales = pack4(w / s[:, None])
    field_a = bf(np.exp(0.2 * np.random.standard_normal(D)) * t)
    field_b = bf(np.exp(0.2 * np.random.standard_normal(D)) / t)
    return {"left_words": left_words, "left_scales": left_scales,
            "right_words": right_words, "right_scales": right_scales,
            "field_a": field_a, "field_b": field_b}


def reference(left_words, left_scales, right_words, right_scales, field_a, field_b):
    left = unpack4(left_words, left_scales)
    right = unpack4(right_words, right_scales)
    P = left.T @ right
    S = P / np.max(np.abs(P))
    A = S * f64(field_a)
    B = S * f64(field_b)[:, None]
    return mxq(A, 1, "e4m3") @ mxq(B, 0, "e4m3")

@@ -1,0 +1,265 @@
+from contextlib import ExitStack
+
+import concourse.mybir as mybir
+from concourse.masks import make_identity
+
+F32 = mybir.dt.float32
+BF16 = mybir.dt.bfloat16
+I32 = mybir.dt.int32
+U32 = mybir.dt.uint32
+U8 = mybir.dt.uint8
+FP8X4 = mybir.dt.float8_e4m3fn_x4
+FP4X4 = mybir.dt.float4_e2m1fn_x4
+ALU = mybir.AluOpType
+AX = mybir.AxisListType
+ACT = mybir.ActivationFunctionType
+
+D = 1024
+P = 128
+G = 2
+T = 4
+A = 16
+B = 8
+H = 512
+
+FLOPS = 2 * 2 * D * D * D
+
+
+def tile_ising_transfer_fourth_power_s4_kernel(
+    tc, left_words, left_scales, right_words, right_scales, field_a, field_b, out
+):
+    nc = tc.nc
+    with ExitStack() as ctx:
+        keep = ctx.enter_context(tc.tile_pool(name="keep", bufs=1))
+        stage = ctx.enter_context(tc.tile_pool(name="stage", bufs=3))
+        results = ctx.enter_context(tc.tile_pool(name="results", bufs=16))
+        psum = ctx.enter_context(tc.psum_pool(name="psum", bufs=8))
+        ctx.enter_context(tc.manual_schedule())
+
+        def bank():
+            b = psum.tile([P, H], F32, name="bank")
+            return b
+
+        lw = keep.tile([P, G, 2 * D], U8, name="lw", align_bytes=256)
+        rw = keep.tile([P, G, 2 * D], U8, name="rw", align_bytes=256)
+        ls = keep.tile([P, G, D], U8, name="ls", align_bytes=256)
+        rs = keep.tile([P, G, D], U8, name="rs", align_bytes=256)
+        lwp = keep.tile([P, G, 8, 2 * P], U8, name="lwp", align_bytes=256)
+        lsp = keep.tile([P, G, 8, P], U8, name="lsp", align_bytes=256)
+        frow = keep.tile([P, P], BF16, name="frow", align_bytes=256)
+        frow32 = keep.tile([P, P], F32, name="frow32", align_bytes=256)
+        fcol = keep.tile([P, 16], F32, name="fcol", align_bytes=256)
+        ident = keep.tile([P, P], F32, name="ident", align_bytes=256)
+        warm = keep.tile([P, 1], F32, name="warm")
+        rmax = keep.tile([P, 16], F32, name="rmax")
+        rall = keep.tile([P, 1], F32, name="rall")
+        mx = keep.tile([P, 1], F32, name="mx")
+        rm = keep.tile([P, 1], F32, name="rm")
+        p_rows = [keep.tile([P, D], F32, name="p_rows%d" % r, align_bytes=256) for r in range(8)]
+        b_rows = [keep.tile([P, T, D], F32, name="b_rows%d" % g, align_bytes=256) for g in range(G)]
+        b_codes = [[keep.tile([P, H], U32, name="b_codes%d%d" % (g, h), align_bytes=256) for h in range(2)] for g in range(G)]
+        b_scales = [[keep.tile([P, H], U8, name="b_scales%d%d" % (g, h), align_bytes=256) for h in range(2)] for g in range(G)]
+        b_grp = [[keep.tile([P, H, T], BF16, name="b_grp%d%d" % (g, h), align_bytes=256) for h in range(2)] for g in range(G)]
+        a_codes = [keep.tile([P, G * P], U32, name="a_codes%d" % r, align_bytes=256) for r in range(8)]
+        a_scales = [keep.tile([P, G * P], U8, name="a_scales%d" % r, align_bytes=256) for r in range(8)]
+
+        nc.vector.memset(ls[:].rearrange("p g n -> p (g n)").bitcast(I32), 0)
+        nc.gpsimd.memset(rs[:].rearrange("p g n -> p (g n)").bitcast(I32), 0)
+        nc.vector.memset(frow32[:], 0.0)
+        nc.vector.memset(warm[:], 0.0)
+
+        def load_words(dst, src, half):
+            cols = slice(half * D, (half + 1) * D)
+            nc.sync.dma_start(out=dst[:, :, cols].bitcast(I32), in_=src[:, :, cols].rearrange("g p n -> p g n").bitcast(I32))
+
+        load_words(lw, left_words, 0)
+        load_words(rw, right_words, 0)
+        load_words(rw, right_words, 1)
+        load_words(lw, left_words, 1)
+        for i, f in enumerate((field_a, field_b)):
+            fv = f.rearrange("(g a t b) -> g t a b", g=G, a=A, t=T, b=B)
+            for g in range(G):
+                row = 8 * i + 4 * g
+                nc.scalar.dma_start(out=frow[row : row + 4, :].rearrange("t (a b) -> t a b", b=B), in_=fv[g])
+        for dst, src in ((ls, left_scales), (rs, right_scales)):
+            for q in range(4):
+                nc.scalar.dma_start(
+                    out=dst[32 * q : 32 * q + 4, :, :].bitcast(I32),
+                    in_=src[:, 4 * q : 4 * q + 4, :].rearrange("g q n -> q g n").bitcast(I32),
+                )
+        nc.scalar.activation(out=warm[:], in_=warm[:], func=ACT.Copy)
+        make_identity(nc, ident[:])
+
+        def permute(gc):
+            for gk in range(G):
+                nc.vector.tensor_copy(
+                    out=lsp[:, gk, 4 * gc : 4 * gc + 4, :].rearrange("p r n -> p (r n)").bitcast(I32).rearrange("p (t a b) -> p t a b", t=T, a=A),
+                    in_=ls[:, gk, gc * H : (gc + 1) * H].bitcast(I32).rearrange("p (a t b) -> p t a b", t=T, a=A),
+                )
+            for gk in range(G):
+                nc.vector.tensor_copy(
+                    out=lwp[:, gk, 4 * gc : 4 * gc + 4, :].rearrange("p r n -> p (r n)").bitcast(I32).rearrange("p (t a b) -> p t a b", t=T, a=A),
+                    in_=lw[:, gk, gc * D : (gc + 1) * D].bitcast(I32).rearrange("p (a t b) -> p t a b", t=T, a=A),
+                )
+
+        def first_product(r, h):
+            acc = bank()
+            for gk in range(G):
+                nc.tensor.matmul_mx(
+                    out=acc[:],
+                    lhsT=lwp[:, gk, r, :].bitcast(FP4X4),
+                    lhsT_scale=lsp[:, gk, r, :],
+                    rhs=rw[:, gk, h * D : (h + 1) * D].bitcast(FP4X4),
+                    rhs_scale=rs[:, gk, h * H : (h + 1) * H],
+                    start=(gk == 0),
+                    stop=(gk == 1),
+                )
+            return acc
+
+        def half_rows(r, h):
+            return p_rows[r][:, h * H : (h + 1) * H]
+
+        def hold(r, h, acc):
+            nc.scalar.copy(
+                out=half_rows(r, h).rearrange("p (t a b) -> p t a b", t=T, a=A),
+                in_=acc[:].rearrange("p (a t b) -> p t a b", t=T, a=A),
+            )
+
+        def largest(r, h, k):
+            nc.vector.tensor_reduce(out=rmax[:, k : k + 1], in_=half_rows(r, h), axis=AX.X, op=ALU.max, apply_absolute_value=True)
+
+        def field_rows(r, h):
+            nc.gpsimd.tensor_scalar(
+                out=b_rows[r // 4][:, r % 4, h * H : (h + 1) * H].rearrange("p (a t b) -> p a t b", t=T, a=A),
+                in0=half_rows(r, h).rearrange("p (t a b) -> p a t b", t=T, a=A),
+                scalar1=fcol[:, 8 + r : 9 + r],
+                scalar2=0.0,
+                op0=ALU.mult,
+                op1=ALU.add,
+            )
+
+        flipped = {}
+
+        def flip(r, g):
+            y = bank()
+            for t in range(T):
+                nc.tensor.transpose(y[:, t * P : (t + 1) * P], p_rows[r][:, g * H + t * P : g * H + (t + 1) * P], ident[:])
+            flipped[r, g] = y
+
+        def b_args(g, h, n0, n):
+            return (
+                b_grp[g][h][:, n0 : n0 + n, :],
+                b_rows[g][:, :, h * H + n0 : h * H + n0 + n].rearrange("p t n -> p n t"),
+            )
+
+        def b_group_vector(g, h, n0=0, n=H):
+            o, i = b_args(g, h, n0, n)
+            nc.vector.tensor_scalar(out=o, in0=i, scalar1=rm[:, 0:1], scalar2=None, op0=ALU.mult)
+
+        def b_group_scalar(g, h, n0=0, n=H):
+            o, i = b_args(g, h, n0, n)
+            nc.scalar.activation(out=o, in_=i, func=ACT.Copy, scale=rm[:, 0:1])
+
+        def b_group_gpsimd(g, h, n0=0, n=H):
+            o, i = b_args(g, h, n0, n)
+            nc.gpsimd.tensor_scalar(out=o, in0=i, scalar1=rm[:, 0:1], scalar2=0.0, op0=ALU.mult, op1=ALU.add)
+
+        def b_quantize(g, h):
+            nc.vector.quantize_mx(out=b_codes[g][h][:].bitcast(FP8X4), scales=b_scales[g][h][:], in_=b_grp[g][h][:].rearrange("p n t -> p (n t)"))
+
+        a_grp = {}
+
+        def a_group(r, g):
+            if g == 0:
+                tile_a = stage.tile([P, G, P, T], BF16, name="a_grp", align_bytes=256)
+                a_grp[r] = tile_a
+            nc.vector.scalar_tensor_tensor(
+                out=a_grp[r][:, g, :, :],
+                in0=flipped[r, g][:].rearrange("p (t n) -> p n t", t=T),
+                scalar=rm[:, 0:1],
+                in1=fcol[:, 4 * g : 4 * g + 4].unsqueeze(1).to_broadcast([P, P, T]),
+                op0=ALU.mult,
+                op1=ALU.mult,
+            )
+
+        def a_quantize(r):
+            nc.vector.quantize_mx(out=a_codes[r][:].bitcast(FP8X4), scales=a_scales[r][:], in_=a_grp[r][:].rearrange("p g n t -> p (g n t)"))
+
+        out_rows = out.rearrange("(g a t b) n -> g t a b n", g=G, a=A, t=T, b=B)
+
+        def product(r, h, engine=None):
+            acc = bank()
+            for g in range(G):
+                nc.tensor.matmul_mx(
+                    out=acc[:],
+                    lhsT=a_codes[r][:, g * P : (g + 1) * P].bitcast(FP8X4),
+                    lhsT_scale=a_scales[r][:, g * P : (g + 1) * P],
+                    rhs=b_codes[g][h][:].bitcast(FP8X4),
+                    rhs_scale=b_scales[g][h][:],
+                    start=(g == 0),
+                    stop=(g == 1),
+                )
+            res = results.tile([P, H], F32, name="res", align_bytes=256)
+            if engine == "v":
+                nc.vector.tensor_copy(out=res[:], in_=acc[:])
+            else:
+                nc.scalar.copy(out=res[:], in_=acc[:])
+            nc.sync.dma_start(out=out_rows[r // 4, r % 4][:, :, h * H : (h + 1) * H], in_=res[:])
+
+        blocks = [(4 * gc + t, h) for gc in range(G) for h in range(2) for t in range(T)]
+        permute(0)
+        nc.vector.tensor_copy(out=frow32[0:16, :], in_=frow[0:16, :])
+        for k, (r, h) in enumerate(blocks):
+            acc = first_product(r, h)
+            hold(r, h, acc)
+            largest(r, h, k)
+            if k == 0:
+                fb = bank()
+                nc.tensor.transpose(fb[:, 0:P], frow32[:], ident[:])
+                nc.vector.tensor_copy(out=fcol[:], in_=fb[:, 0:16])
+            field_rows(r, h)
+            if k == 3:
+                permute(1)
+        for r in range(3):
+            for g in range(G):
+                flip(r, g)
+        nc.vector.tensor_reduce(out=rall[:], in_=rmax[:], axis=AX.X, op=ALU.max)
+        mb = bank()
+        nc.tensor.transpose(mb[:, 0:P], rall[:, 0:1].to_broadcast([P, P]), ident[:])
+        nc.vector.tensor_reduce(out=mx[:], in_=mb[:, 0:P], axis=AX.X, op=ALU.max)
+        nc.vector.reciprocal(out=rm[:], in_=mx[:])
+        b_group_scalar(0, 0)
+        b_group_gpsimd(0, 1)
+        b_group_scalar(1, 1)
+        b_group_vector(1, 0)
+        flip(3, 0)
+        flip(3, 1)
+        a_group(0, 0)
+        b_quantize(1, 0)
+        a_group(0, 1)
+        b_quantize(0, 0)
+        a_quantize(0)
+        product(0, 0)
+        a_group(1, 0)
+        a_group(1, 1)
+        b_quantize(0, 1)
+        b_quantize(1, 1)
+        a_quantize(1)
+        product(0, 1)
+        product(1, 0)
+        flip(4, 0)
+        flip(4, 1)
+        product(1, 1)
+        for r in range(2, 8):
+            a_group(r, 0)
+            a_group(r, 1)
+            if r > 2:
+                a_quantize(r - 1)
+                product(r - 1, 0)
+                if r + 2 < 8:
+                    flip(r + 2, 0)
+                    flip(r + 2, 1)
+                product(r - 1, 1)
+        a_quantize(7)
+        product(7, 0)
+        product(7, 1, "v")

@@ -33,8 +33,13 @@ def tile_ising_transfer_fourth_power_s4_kernel(
         keep = ctx.enter_context(tc.tile_pool(name="keep", bufs=1))
         stage = ctx.enter_context(tc.tile_pool(name="stage", bufs=3))
         results = ctx.enter_context(tc.tile_pool(name="results", bufs=16))
-        psum = ctx.enter_context(tc.psum_pool(name="psum", bufs=8))
+        psum = ctx.enter_context(tc.psum_pool(name="psum", bufs=7))
+        misc = ctx.enter_context(tc.psum_pool(name="misc", bufs=1))
         ctx.enter_context(tc.manual_schedule())
+
+        def misc_bank():
+            mb = misc.tile([P, H], F32, name="mbank")
+            return mb
 
         def bank():
             b = psum.tile([P, H], F32, name="bank")
@@ -46,16 +51,17 @@ def tile_ising_transfer_fourth_power_s4_kernel(
         rs = keep.tile([P, G, D], U8, name="rs", align_bytes=256)
         lwp = keep.tile([P, G, 8, 2 * P], U8, name="lwp", align_bytes=256)
         lsp = keep.tile([P, G, 8, P], U8, name="lsp", align_bytes=256)
-        frow = keep.tile([P, P], BF16, name="frow", align_bytes=256)
-        frow32 = keep.tile([P, P], F32, name="frow32", align_bytes=256)
+        frow = keep.tile([P, 2 * P], BF16, name="frow", align_bytes=256)
+        frow32 = keep.tile([P, 2 * P], F32, name="frow32", align_bytes=256)
         fcol = keep.tile([P, 16], F32, name="fcol", align_bytes=256)
         ident = keep.tile([P, P], F32, name="ident", align_bytes=256)
         warm = keep.tile([P, 1], F32, name="warm")
-        rmax = keep.tile([P, 16], F32, name="rmax")
+        wz = keep.tile([P, H], BF16, name="wz", align_bytes=256)
+        a_raw = keep.tile([P, T, H], F32, name="a_raw", align_bytes=256)
         rall = keep.tile([P, 1], F32, name="rall")
         mx = keep.tile([P, 1], F32, name="mx")
         rm = keep.tile([P, 1], F32, name="rm")
-        p_rows = [keep.tile([P, D], F32, name="p_rows%d" % r, align_bytes=256) for r in range(8)]
+        p_rows = [keep.tile([P, D + 16], F32, name="p_rows%d" % r, align_bytes=256) for r in range(8)]
         b_rows = [keep.tile([P, T, D], F32, name="b_rows%d" % g, align_bytes=256) for g in range(G)]
         b_codes = [[keep.tile([P, H], U32, name="b_codes%d%d" % (g, h), align_bytes=256) for h in range(2)] for g in range(G)]
         b_scales = [[keep.tile([P, H], U8, name="b_scales%d%d" % (g, h), align_bytes=256) for h in range(2)] for g in range(G)]
@@ -63,32 +69,42 @@ def tile_ising_transfer_fourth_power_s4_kernel(
         a_codes = [keep.tile([P, G * P], U32, name="a_codes%d" % r, align_bytes=256) for r in range(8)]
         a_scales = [keep.tile([P, G * P], U8, name="a_scales%d" % r, align_bytes=256) for r in range(8)]
 
-        nc.vector.memset(ls[:].rearrange("p g n -> p (g n)").bitcast(I32), 0)
-        nc.gpsimd.memset(rs[:].rearrange("p g n -> p (g n)").bitcast(I32), 0)
-        nc.vector.memset(frow32[:], 0.0)
         nc.vector.memset(warm[:], 0.0)
+        nc.vector.memset(ls[:].rearrange("p g n -> p (g n)").bitcast(I32), 0)
+        nc.vector.memset(rs[:].rearrange("p g n -> p (g n)").bitcast(I32), 0)
+        nc.vector.memset(wz[:], 0.0)
+        nc.vector.memset(frow32[:], 0.0)
 
         def load_words(dst, src, half):
             cols = slice(half * D, (half + 1) * D)
             nc.sync.dma_start(out=dst[:, :, cols].bitcast(I32), in_=src[:, :, cols].rearrange("g p n -> p g n").bitcast(I32))
 
+        def load_scales(engine, dst, src, q):
+            engine.dma_start(
+                out=dst[32 * q : 32 * q + 4, :, :].bitcast(I32),
+                in_=src[:, 4 * q : 4 * q + 4, :].rearrange("g q n -> q g n").bitcast(I32),
+            )
+
+        make_identity(nc, ident[:])
+        for i, f in enumerate((field_a, field_b)):
+            nc.sync.dma_start(
+                out=frow[4 * i : 4 * i + 4, :].rearrange("t (c b) -> t c b", b=B),
+                in_=f.rearrange("(c t b) -> t c b", t=T, b=B),
+            )
         load_words(lw, left_words, 0)
         load_words(rw, right_words, 0)
-        load_words(rw, right_words, 1)
+        for q in range(4):
+            load_scales(nc.scalar, ls, left_scales, q)
+        for q in range(2):
+            load_scales(nc.scalar, rs, right_scales, q)
         load_words(lw, left_words, 1)
-        for i, f in enumerate((field_a, field_b)):
-            fv = f.rearrange("(g a t b) -> g t a b", g=G, a=A, t=T, b=B)
-            for g in range(G):
-                row = 8 * i + 4 * g
-                nc.scalar.dma_start(out=frow[row : row + 4, :].rearrange("t (a b) -> t a b", b=B), in_=fv[g])
-        for dst, src in ((ls, left_scales), (rs, right_scales)):
-            for q in range(4):
-                nc.scalar.dma_start(
-                    out=dst[32 * q : 32 * q + 4, :, :].bitcast(I32),
-                    in_=src[:, 4 * q : 4 * q + 4, :].rearrange("g q n -> q g n").bitcast(I32),
-                )
+        load_words(rw, right_words, 1)
         nc.scalar.activation(out=warm[:], in_=warm[:], func=ACT.Copy)
-        make_identity(nc, ident[:])
+        for q in range(2, 4):
+            load_scales(nc.gpsimd, rs, right_scales, q)
+        wb = misc_bank()
+        for i in range(4):
+            nc.tensor.matmul(wb[:], wz[:, 0:P], wz[:], start=True, stop=True)
 
         def permute(gc):
             for gk in range(G):
@@ -125,14 +141,16 @@ def tile_ising_transfer_fourth_power_s4_kernel(
                 in_=acc[:].rearrange("p (a t b) -> p t a b", t=T, a=A),
             )
 
+        rmax = p_rows[7]
+
         def largest(r, h, k):
-            nc.vector.tensor_reduce(out=rmax[:, k : k + 1], in_=half_rows(r, h), axis=AX.X, op=ALU.max, apply_absolute_value=True)
+            nc.vector.tensor_reduce(out=rmax[:, D + k : D + k + 1], in_=half_rows(r, h), axis=AX.X, op=ALU.max, apply_absolute_value=True)
 
         def field_rows(r, h):
             nc.gpsimd.tensor_scalar(
                 out=b_rows[r // 4][:, r % 4, h * H : (h + 1) * H].rearrange("p (a t b) -> p a t b", t=T, a=A),
                 in0=half_rows(r, h).rearrange("p (t a b) -> p a t b", t=T, a=A),
-                scalar1=fcol[:, 8 + r : 9 + r],
+                scalar1=fcol[:, 8 * (r // 4) + 4 + r % 4 : 8 * (r // 4) + 5 + r % 4],
                 scalar2=0.0,
                 op0=ALU.mult,
                 op1=ALU.add,
@@ -164,8 +182,18 @@ def tile_ising_transfer_fourth_power_s4_kernel(
             o, i = b_args(g, h, n0, n)
             nc.gpsimd.tensor_scalar(out=o, in0=i, scalar1=rm[:, 0:1], scalar2=0.0, op0=ALU.mult, op1=ALU.add)
 
-        def b_quantize(g, h):
-            nc.vector.quantize_mx(out=b_codes[g][h][:].bitcast(FP8X4), scales=b_scales[g][h][:], in_=b_grp[g][h][:].rearrange("p n t -> p (n t)"))
+        def b_quantize(g, h, n0=0, n=H):
+            nc.vector.quantize_mx(
+                out=b_codes[g][h][:, n0 : n0 + n].bitcast(FP8X4),
+                scales=b_scales[g][h][:, n0 : n0 + n],
+                in_=b_grp[g][h][:, n0 : n0 + n, :].rearrange("p n t -> p (n t)"),
+            )
+
+        def flip_across(t2):
+            y = bank()
+            for t in range(T):
+                nc.tensor.transpose(y[:, t * P : (t + 1) * P], p_rows[4 + t][:, t2 * P : (t2 + 1) * P], ident[:])
+            nc.scalar.activation(out=a_raw[:, t2, :], in_=y[:], func=ACT.Copy, scale=fcol[:, t2 : t2 + 1])
 
         a_grp = {}
 
@@ -173,11 +201,20 @@ def tile_ising_transfer_fourth_power_s4_kernel(
             if g == 0:
                 tile_a = stage.tile([P, G, P, T], BF16, name="a_grp", align_bytes=256)
                 a_grp[r] = tile_a
+            if r >= 4 and g == 0:
+                nc.vector.tensor_scalar(
+                    out=a_grp[r][:, g, :, :],
+                    in0=a_raw[:, :, (r - 4) * P : (r - 3) * P].rearrange("p t n -> p n t"),
+                    scalar1=rm[:, 0:1],
+                    scalar2=None,
+                    op0=ALU.mult,
+                )
+                return
             nc.vector.scalar_tensor_tensor(
                 out=a_grp[r][:, g, :, :],
                 in0=flipped[r, g][:].rearrange("p (t n) -> p n t", t=T),
                 scalar=rm[:, 0:1],
-                in1=fcol[:, 4 * g : 4 * g + 4].unsqueeze(1).to_broadcast([P, P, T]),
+                in1=fcol[:, 8 * g : 8 * g + 4].unsqueeze(1).to_broadcast([P, P, T]),
                 op0=ALU.mult,
                 op1=ALU.mult,
             )
@@ -187,79 +224,106 @@ def tile_ising_transfer_fourth_power_s4_kernel(
 
         out_rows = out.rearrange("(g a t b) n -> g t a b n", g=G, a=A, t=T, b=B)
 
-        def product(r, h, engine=None):
+        def product(r, h, engine="s", n0=0, n=H):
             acc = bank()
             for g in range(G):
                 nc.tensor.matmul_mx(
-                    out=acc[:],
+                    out=acc[:, 0:n],
                     lhsT=a_codes[r][:, g * P : (g + 1) * P].bitcast(FP8X4),
                     lhsT_scale=a_scales[r][:, g * P : (g + 1) * P],
-                    rhs=b_codes[g][h][:].bitcast(FP8X4),
-                    rhs_scale=b_scales[g][h][:],
+                    rhs=b_codes[g][h][:, n0 : n0 + n].bitcast(FP8X4),
+                    rhs_scale=b_scales[g][h][:, n0 : n0 + n],
                     start=(g == 0),
                     stop=(g == 1),
                 )
             res = results.tile([P, H], F32, name="res", align_bytes=256)
-            if engine == "v":
-                nc.vector.tensor_copy(out=res[:], in_=acc[:])
-            else:
-                nc.scalar.copy(out=res[:], in_=acc[:])
-            nc.sync.dma_start(out=out_rows[r // 4, r % 4][:, :, h * H : (h + 1) * H], in_=res[:])
+            pieces = [(engine, 0, n)] if len(engine) == 1 else [(engine[0], 0, n // 2), (engine[1], n // 2, n)]
+            for e, c0, c1 in pieces:
+                if e == "v":
+                    nc.vector.tensor_copy(out=res[:, c0:c1], in_=acc[:, c0:c1])
+                else:
+                    nc.scalar.copy(out=res[:, c0:c1], in_=acc[:, c0:c1])
+                nc.sync.dma_start(out=out_rows[r // 4, r % 4][:, :, h * H + n0 + c0 : h * H + n0 + c1], in_=res[:, c0:c1])
 
-        blocks = [(4 * gc + t, h) for gc in range(G) for h in range(2) for t in range(T)]
+        blocks = [(4 * gc + t, h) for h in range(2) for gc in range(G) for t in range(T)]
+        nc.vector.tensor_copy(out=frow32[0:8, :], in_=frow[0:8, :])
+        fb = misc_bank()
+        for g in range(G):
+            nc.tensor.transpose(fb[:, g * P : (g + 1) * P], frow32[:, g * P : (g + 1) * P], ident[:])
+        wb2 = bank()
+        for i in range(5):
+            nc.tensor.matmul(wb2[:], wz[:, 0:P], wz[:], start=True, stop=True)
+        nc.vector.tensor_copy(out=fcol[:].rearrange("p (g x) -> p g x", g=G), in_=fb[:, 0 : 2 * P].rearrange("p (g x) -> p g x", g=G)[:, :, 0:8])
         permute(0)
-        nc.vector.tensor_copy(out=frow32[0:16, :], in_=frow[0:16, :])
+        permute(1)
         for k, (r, h) in enumerate(blocks):
             acc = first_product(r, h)
-            hold(r, h, acc)
-            largest(r, h, k)
-            if k == 0:
-                fb = bank()
-                nc.tensor.transpose(fb[:, 0:P], frow32[:], ident[:])
-                nc.vector.tensor_copy(out=fcol[:], in_=fb[:, 0:16])
+            if k < 15:
+                hold(r, h, acc)
+                largest(r, h, k)
+            else:
+                for i in range(2):
+                    nc.scalar.copy(
+                        out=p_rows[r][:, H + i * 256 : H + (i + 1) * 256].rearrange("p (t a b) -> p t a b", t=2, a=A),
+                        in_=acc[:].rearrange("p (a t b) -> p t a b", t=T, a=A)[:, 2 * i : 2 * i + 2],
+                    )
+                nc.vector.tensor_reduce(out=rmax[:, D + 15 : D + 16], in_=p_rows[r][:, H : H + 256], axis=AX.X, op=ALU.max, apply_absolute_value=True)
             field_rows(r, h)
-            if k == 3:
-                permute(1)
-        for r in range(3):
-            for g in range(G):
-                flip(r, g)
-        nc.vector.tensor_reduce(out=rall[:], in_=rmax[:], axis=AX.X, op=ALU.max)
-        mb = bank()
+        for t in range(T):
+            flip_across(t)
+        flip(0, 0)
+        nc.vector.tensor_reduce(out=rall[:], in_=p_rows[7][:, H + 256 : D + 16], axis=AX.X, op=ALU.max, apply_absolute_value=True)
+        mb = misc_bank()
         nc.tensor.transpose(mb[:, 0:P], rall[:, 0:1].to_broadcast([P, P]), ident[:])
         nc.vector.tensor_reduce(out=mx[:], in_=mb[:, 0:P], axis=AX.X, op=ALU.max)
         nc.vector.reciprocal(out=rm[:], in_=mx[:])
+        flip(0, 1)
+        flip(1, 0)
+        flip(1, 1)
+        flip(2, 0)
+        flip(2, 1)
         b_group_scalar(0, 0)
-        b_group_gpsimd(0, 1)
-        b_group_scalar(1, 1)
         b_group_vector(1, 0)
-        flip(3, 0)
-        flip(3, 1)
+        b_group_scalar(0, 1)
+        b_group_scalar(1, 1)
         a_group(0, 0)
-        b_quantize(1, 0)
         a_group(0, 1)
         b_quantize(0, 0)
+        b_quantize(1, 0)
         a_quantize(0)
         product(0, 0)
         a_group(1, 0)
         a_group(1, 1)
-        b_quantize(0, 1)
-        b_quantize(1, 1)
+        a_group(2, 0)
         a_quantize(1)
-        product(0, 1)
+        a_group(2, 1)
+        flip(3, 0)
+        flip(3, 1)
         product(1, 0)
-        flip(4, 0)
         flip(4, 1)
+        flip(5, 1)
+        b_quantize(0, 1)
+        a_quantize(2)
+        product(2, 0)
+        a_group(3, 0)
+        b_quantize(1, 1)
+        a_group(3, 1)
+        product(0, 1)
         product(1, 1)
-        for r in range(2, 8):
+        flip(6, 1)
+        flip(7, 1)
+        product(2, 1)
+        a_quantize(3)
+        a_group(4, 0)
+        a_group(4, 1)
+        product(3, 0)
+        product(3, 1)
+        for r in range(5, 8):
             a_group(r, 0)
+            a_quantize(r - 1)
             a_group(r, 1)
-            if r > 2:
-                a_quantize(r - 1)
-                product(r - 1, 0)
-                if r + 2 < 8:
-                    flip(r + 2, 0)
-                    flip(r + 2, 1)
-                product(r - 1, 1)
+            product(r - 1, 0)
+            product(r - 1, 1)
         a_quantize(7)
-        product(7, 0)
-        product(7, 1, "v")
+        product(7, 0, "v")
+        product(7, 1, "vs")

@@ -31,19 +31,24 @@ def tile_ising_transfer_fourth_power_s4_kernel(
     nc = tc.nc
     with ExitStack() as ctx:
         keep = ctx.enter_context(tc.tile_pool(name="keep", bufs=1))
-        stage = ctx.enter_context(tc.tile_pool(name="stage", bufs=3))
+        stage = ctx.enter_context(tc.tile_pool(name="stage", bufs=4))
         results = ctx.enter_context(tc.tile_pool(name="results", bufs=16))
-        psum = ctx.enter_context(tc.psum_pool(name="psum", bufs=7))
+        psum = ctx.enter_context(tc.psum_pool(name="psum", bufs=3))
+        turn = ctx.enter_context(tc.psum_pool(name="turn", bufs=4))
         misc = ctx.enter_context(tc.psum_pool(name="misc", bufs=1))
         ctx.enter_context(tc.manual_schedule())
-
-        def misc_bank():
-            mb = misc.tile([P, H], F32, name="mbank")
-            return mb
 
         def bank():
             b = psum.tile([P, H], F32, name="bank")
             return b
+
+        def turn_bank():
+            tb = turn.tile([P, H], F32, name="tbank")
+            return tb
+
+        def misc_bank():
+            mb = misc.tile([P, H], F32, name="mbank")
+            return mb
 
         lw = keep.tile([P, G, 2 * D], U8, name="lw", align_bytes=256)
         rw = keep.tile([P, G, 2 * D], U8, name="rw", align_bytes=256)
@@ -68,16 +73,11 @@ def tile_ising_transfer_fourth_power_s4_kernel(
         b_grp = [[keep.tile([P, H, T], BF16, name="b_grp%d%d" % (g, h), align_bytes=256) for h in range(2)] for g in range(G)]
         a_codes = [keep.tile([P, G * P], U32, name="a_codes%d" % r, align_bytes=256) for r in range(8)]
         a_scales = [keep.tile([P, G * P], U8, name="a_scales%d" % r, align_bytes=256) for r in range(8)]
+        rmax = p_rows[7]
 
-        nc.vector.memset(warm[:], 0.0)
-        nc.vector.memset(ls[:].rearrange("p g n -> p (g n)").bitcast(I32), 0)
-        nc.vector.memset(rs[:].rearrange("p g n -> p (g n)").bitcast(I32), 0)
-        nc.vector.memset(wz[:], 0.0)
-        nc.vector.memset(frow32[:], 0.0)
-
-        def load_words(dst, src, half):
+        def load_words(engine, dst, src, half):
             cols = slice(half * D, (half + 1) * D)
-            nc.sync.dma_start(out=dst[:, :, cols].bitcast(I32), in_=src[:, :, cols].rearrange("g p n -> p g n").bitcast(I32))
+            engine.dma_start(out=dst[:, :, cols].bitcast(I32), in_=src[:, :, cols].rearrange("g p n -> p g n").bitcast(I32))
 
         def load_scales(engine, dst, src, q):
             engine.dma_start(
@@ -85,38 +85,53 @@ def tile_ising_transfer_fourth_power_s4_kernel(
                 in_=src[:, 4 * q : 4 * q + 4, :].rearrange("g q n -> q g n").bitcast(I32),
             )
 
-        make_identity(nc, ident[:])
-        for i, f in enumerate((field_a, field_b)):
-            nc.sync.dma_start(
+        def load_field(engine, i, f):
+            engine.dma_start(
                 out=frow[4 * i : 4 * i + 4, :].rearrange("t (c b) -> t c b", b=B),
                 in_=f.rearrange("(c t b) -> t c b", t=T, b=B),
             )
-        load_words(lw, left_words, 0)
-        load_words(rw, right_words, 0)
+
+        load_words(nc.gpsimd, lw, left_words, 0)
+        load_words(nc.gpsimd, rw, right_words, 0)
+        load_words(nc.gpsimd, lw, left_words, 1)
+        for q in range(4):
+            load_scales(nc.sync, rs, right_scales, q)
+        nc.vector.memset(ls[:].rearrange("p g n -> p (g n)").bitcast(I32), 0)
         for q in range(4):
             load_scales(nc.scalar, ls, left_scales, q)
-        for q in range(2):
-            load_scales(nc.scalar, rs, right_scales, q)
-        load_words(lw, left_words, 1)
-        load_words(rw, right_words, 1)
+        load_field(nc.sync, 0, field_a)
+        load_field(nc.sync, 1, field_b)
+        load_words(nc.sync, rw, right_words, 1)
+        make_identity(nc, ident[:])
+        nc.vector.memset(warm[:], 0.0)
         nc.scalar.activation(out=warm[:], in_=warm[:], func=ACT.Copy)
-        for q in range(2, 4):
-            load_scales(nc.gpsimd, rs, right_scales, q)
-        wb = misc_bank()
-        for i in range(4):
+        nc.vector.memset(wz[:], 0.0)
+        nc.vector.memset(frow32[:], 0.0)
+        wb = bank()
+        for i in range(6):
             nc.tensor.matmul(wb[:], wz[:, 0:P], wz[:], start=True, stop=True)
 
-        def permute(gc):
+
+        def permute_scales(gc):
             for gk in range(G):
                 nc.vector.tensor_copy(
                     out=lsp[:, gk, 4 * gc : 4 * gc + 4, :].rearrange("p r n -> p (r n)").bitcast(I32).rearrange("p (t a b) -> p t a b", t=T, a=A),
                     in_=ls[:, gk, gc * H : (gc + 1) * H].bitcast(I32).rearrange("p (a t b) -> p t a b", t=T, a=A),
                 )
+
+        def permute_words(gc):
             for gk in range(G):
                 nc.vector.tensor_copy(
                     out=lwp[:, gk, 4 * gc : 4 * gc + 4, :].rearrange("p r n -> p (r n)").bitcast(I32).rearrange("p (t a b) -> p t a b", t=T, a=A),
                     in_=lw[:, gk, gc * D : (gc + 1) * D].bitcast(I32).rearrange("p (a t b) -> p t a b", t=T, a=A),
                 )
+
+        def field_columns():
+            nc.vector.tensor_copy(out=frow32[0:8, :], in_=frow[0:8, :])
+            fb = misc_bank()
+            for g in range(G):
+                nc.tensor.transpose(fb[:, g * P : (g + 1) * P], frow32[:, g * P : (g + 1) * P], ident[:])
+            nc.vector.tensor_copy(out=fcol[:].rearrange("p (g x) -> p g x", g=G), in_=fb[:, 0 : 2 * P].rearrange("p (g x) -> p g x", g=G)[:, :, 0:8])
 
         def first_product(r, h):
             acc = bank()
@@ -135,16 +150,14 @@ def tile_ising_transfer_fourth_power_s4_kernel(
         def half_rows(r, h):
             return p_rows[r][:, h * H : (h + 1) * H]
 
-        def hold(r, h, acc):
+        def hold(r, h, acc, t0=0, t1=T):
             nc.scalar.copy(
-                out=half_rows(r, h).rearrange("p (t a b) -> p t a b", t=T, a=A),
-                in_=acc[:].rearrange("p (a t b) -> p t a b", t=T, a=A),
+                out=p_rows[r][:, h * H + t0 * P : h * H + t1 * P].rearrange("p (t a b) -> p t a b", t=t1 - t0, a=A),
+                in_=acc[:].rearrange("p (a t b) -> p t a b", t=T, a=A)[:, t0:t1],
             )
 
-        rmax = p_rows[7]
-
-        def largest(r, h, k):
-            nc.vector.tensor_reduce(out=rmax[:, D + k : D + k + 1], in_=half_rows(r, h), axis=AX.X, op=ALU.max, apply_absolute_value=True)
+        def largest(r, c0, c1, out):
+            nc.vector.tensor_reduce(out=out, in_=p_rows[r][:, c0:c1], axis=AX.X, op=ALU.max, apply_absolute_value=True)
 
         def field_rows(r, h):
             nc.gpsimd.tensor_scalar(
@@ -159,28 +172,26 @@ def tile_ising_transfer_fourth_power_s4_kernel(
         flipped = {}
 
         def flip(r, g):
-            y = bank()
+            y = turn_bank()
             for t in range(T):
                 nc.tensor.transpose(y[:, t * P : (t + 1) * P], p_rows[r][:, g * H + t * P : g * H + (t + 1) * P], ident[:])
             flipped[r, g] = y
 
-        def b_args(g, h, n0, n):
-            return (
-                b_grp[g][h][:, n0 : n0 + n, :],
-                b_rows[g][:, :, h * H + n0 : h * H + n0 + n].rearrange("p t n -> p n t"),
-            )
+        def flip_across(t2):
+            y = turn_bank()
+            for t in range(T):
+                nc.tensor.transpose(y[:, t * P : (t + 1) * P], p_rows[4 + t][:, t2 * P : (t2 + 1) * P], ident[:])
+            nc.scalar.activation(out=a_raw[:, t2, :], in_=y[:], func=ACT.Copy, scale=fcol[:, t2 : t2 + 1])
 
-        def b_group_vector(g, h, n0=0, n=H):
-            o, i = b_args(g, h, n0, n)
-            nc.vector.tensor_scalar(out=o, in0=i, scalar1=rm[:, 0:1], scalar2=None, op0=ALU.mult)
-
-        def b_group_scalar(g, h, n0=0, n=H):
-            o, i = b_args(g, h, n0, n)
-            nc.scalar.activation(out=o, in_=i, func=ACT.Copy, scale=rm[:, 0:1])
-
-        def b_group_gpsimd(g, h, n0=0, n=H):
-            o, i = b_args(g, h, n0, n)
-            nc.gpsimd.tensor_scalar(out=o, in0=i, scalar1=rm[:, 0:1], scalar2=0.0, op0=ALU.mult, op1=ALU.add)
+        def b_group(engine, g, h, n0=0, n=H):
+            o = b_grp[g][h][:, n0 : n0 + n, :]
+            i = b_rows[g][:, :, h * H + n0 : h * H + n0 + n].rearrange("p t n -> p n t")
+            if engine == "s":
+                nc.scalar.activation(out=o, in_=i, func=ACT.Copy, scale=rm[:, 0:1])
+            elif engine == "v":
+                nc.vector.tensor_scalar(out=o, in0=i, scalar1=rm[:, 0:1], scalar2=None, op0=ALU.mult)
+            else:
+                nc.gpsimd.tensor_scalar(out=o, in0=i, scalar1=rm[:, 0:1], scalar2=0.0, op0=ALU.mult, op1=ALU.add)
 
         def b_quantize(g, h, n0=0, n=H):
             nc.vector.quantize_mx(
@@ -189,16 +200,10 @@ def tile_ising_transfer_fourth_power_s4_kernel(
                 in_=b_grp[g][h][:, n0 : n0 + n, :].rearrange("p n t -> p (n t)"),
             )
 
-        def flip_across(t2):
-            y = bank()
-            for t in range(T):
-                nc.tensor.transpose(y[:, t * P : (t + 1) * P], p_rows[4 + t][:, t2 * P : (t2 + 1) * P], ident[:])
-            nc.scalar.activation(out=a_raw[:, t2, :], in_=y[:], func=ACT.Copy, scale=fcol[:, t2 : t2 + 1])
-
         a_grp = {}
 
         def a_group(r, g):
-            if g == 0:
+            if r not in a_grp:
                 tile_a = stage.tile([P, G, P, T], BF16, name="a_grp", align_bytes=256)
                 a_grp[r] = tile_a
             if r >= 4 and g == 0:
@@ -224,55 +229,53 @@ def tile_ising_transfer_fourth_power_s4_kernel(
 
         out_rows = out.rearrange("(g a t b) n -> g t a b n", g=G, a=A, t=T, b=B)
 
-        def product(r, h, engine="s", n0=0, n=H):
+        def product(r, h, engines="s"):
             acc = bank()
             for g in range(G):
                 nc.tensor.matmul_mx(
-                    out=acc[:, 0:n],
+                    out=acc[:],
                     lhsT=a_codes[r][:, g * P : (g + 1) * P].bitcast(FP8X4),
                     lhsT_scale=a_scales[r][:, g * P : (g + 1) * P],
-                    rhs=b_codes[g][h][:, n0 : n0 + n].bitcast(FP8X4),
-                    rhs_scale=b_scales[g][h][:, n0 : n0 + n],
+                    rhs=b_codes[g][h][:].bitcast(FP8X4),
+                    rhs_scale=b_scales[g][h][:],
                     start=(g == 0),
                     stop=(g == 1),
                 )
             res = results.tile([P, H], F32, name="res", align_bytes=256)
-            pieces = [(engine, 0, n)] if len(engine) == 1 else [(engine[0], 0, n // 2), (engine[1], n // 2, n)]
-            for e, c0, c1 in pieces:
+            n = H // len(engines)
+            for i, e in enumerate(engines):
+                cols = slice(i * n, (i + 1) * n)
                 if e == "v":
-                    nc.vector.tensor_copy(out=res[:, c0:c1], in_=acc[:, c0:c1])
+                    nc.vector.tensor_copy(out=res[:, cols], in_=acc[:, cols])
                 else:
-                    nc.scalar.copy(out=res[:, c0:c1], in_=acc[:, c0:c1])
-                nc.sync.dma_start(out=out_rows[r // 4, r % 4][:, :, h * H + n0 + c0 : h * H + n0 + c1], in_=res[:, c0:c1])
+                    nc.scalar.copy(out=res[:, cols], in_=acc[:, cols])
+                nc.sync.dma_start(out=out_rows[r // 4, r % 4][:, :, h * H + i * n : h * H + (i + 1) * n], in_=res[:, cols])
 
         blocks = [(4 * gc + t, h) for h in range(2) for gc in range(G) for t in range(T)]
-        nc.vector.tensor_copy(out=frow32[0:8, :], in_=frow[0:8, :])
-        fb = misc_bank()
-        for g in range(G):
-            nc.tensor.transpose(fb[:, g * P : (g + 1) * P], frow32[:, g * P : (g + 1) * P], ident[:])
-        wb2 = bank()
-        for i in range(5):
-            nc.tensor.matmul(wb2[:], wz[:, 0:P], wz[:], start=True, stop=True)
-        nc.vector.tensor_copy(out=fcol[:].rearrange("p (g x) -> p g x", g=G), in_=fb[:, 0 : 2 * P].rearrange("p (g x) -> p g x", g=G)[:, :, 0:8])
-        permute(0)
-        permute(1)
+        permute_scales(0)
+        permute_words(0)
+        permute_scales(1)
+        permute_words(1)
         for k, (r, h) in enumerate(blocks):
             acc = first_product(r, h)
+            if k == 1:
+                field_columns()
             if k < 15:
                 hold(r, h, acc)
-                largest(r, h, k)
             else:
-                for i in range(2):
-                    nc.scalar.copy(
-                        out=p_rows[r][:, H + i * 256 : H + (i + 1) * 256].rearrange("p (t a b) -> p t a b", t=2, a=A),
-                        in_=acc[:].rearrange("p (a t b) -> p t a b", t=T, a=A)[:, 2 * i : 2 * i + 2],
-                    )
-                nc.vector.tensor_reduce(out=rmax[:, D + 15 : D + 16], in_=p_rows[r][:, H : H + 256], axis=AX.X, op=ALU.max, apply_absolute_value=True)
-            field_rows(r, h)
+                hold(r, h, acc, 0, 2)
+                hold(r, h, acc, 2, 4)
+            if k >= 1:
+                j = k - 1
+                r2, h2 = blocks[j]
+                largest(r2, h2 * H, h2 * H + H, rmax[:, D + j : D + j + 1])
+                field_rows(r2, h2)
+        field_rows(7, 1)
+        largest(7, H, H + 256, rmax[:, D + 15 : D + 16])
+        largest(7, H + 256, D + 16, rall[:])
         for t in range(T):
             flip_across(t)
         flip(0, 0)
-        nc.vector.tensor_reduce(out=rall[:], in_=p_rows[7][:, H + 256 : D + 16], axis=AX.X, op=ALU.max, apply_absolute_value=True)
         mb = misc_bank()
         nc.tensor.transpose(mb[:, 0:P], rall[:, 0:1].to_broadcast([P, P]), ident[:])
         nc.vector.tensor_reduce(out=mx[:], in_=mb[:, 0:P], axis=AX.X, op=ALU.max)
@@ -280,44 +283,45 @@ def tile_ising_transfer_fourth_power_s4_kernel(
         flip(0, 1)
         flip(1, 0)
         flip(1, 1)
-        flip(2, 0)
-        flip(2, 1)
-        b_group_scalar(0, 0)
-        b_group_vector(1, 0)
-        b_group_scalar(0, 1)
-        b_group_scalar(1, 1)
+        b_group("s", 0, 0)
+        b_group("g", 1, 0, 0, 256)
+        b_group("g", 1, 0, 256, 256)
+        b_group("s", 0, 1)
+        b_group("s", 1, 1)
         a_group(0, 0)
         a_group(0, 1)
+        flip(2, 0)
+        flip(2, 1)
+        a_group(1, 0)
+        a_group(1, 1)
+        flip(3, 0)
+        flip(3, 1)
         b_quantize(0, 0)
         b_quantize(1, 0)
         a_quantize(0)
-        product(0, 0)
-        a_group(1, 0)
-        a_group(1, 1)
-        a_group(2, 0)
         a_quantize(1)
-        a_group(2, 1)
-        flip(3, 0)
-        flip(3, 1)
+        product(0, 0)
         product(1, 0)
+        a_group(2, 0)
+        a_group(2, 1)
         flip(4, 1)
         flip(5, 1)
         b_quantize(0, 1)
         a_quantize(2)
         product(2, 0)
         a_group(3, 0)
-        b_quantize(1, 1)
         a_group(3, 1)
-        product(0, 1)
-        product(1, 1)
         flip(6, 1)
         flip(7, 1)
+        b_quantize(1, 1)
+        product(0, 1)
+        product(1, 1)
         product(2, 1)
         a_quantize(3)
-        a_group(4, 0)
-        a_group(4, 1)
         product(3, 0)
         product(3, 1)
+        a_group(4, 0)
+        a_group(4, 1)
         for r in range(5, 8):
             a_group(r, 0)
             a_quantize(r - 1)

@@ -31,7 +31,7 @@ def tile_ising_transfer_fourth_power_s4_kernel(
     nc = tc.nc
     with ExitStack() as ctx:
         keep = ctx.enter_context(tc.tile_pool(name="keep", bufs=1))
-        stage = ctx.enter_context(tc.tile_pool(name="stage", bufs=4))
+        stage = ctx.enter_context(tc.tile_pool(name="stage", bufs=8))
         results = ctx.enter_context(tc.tile_pool(name="results", bufs=16))
         psum = ctx.enter_context(tc.psum_pool(name="psum", bufs=3))
         turn = ctx.enter_context(tc.psum_pool(name="turn", bufs=4))
@@ -91,26 +91,31 @@ def tile_ising_transfer_fourth_power_s4_kernel(
                 in_=f.rearrange("(c t b) -> t c b", t=T, b=B),
             )
 
-        load_words(nc.gpsimd, lw, left_words, 0)
-        load_words(nc.gpsimd, rw, right_words, 0)
-        load_words(nc.gpsimd, lw, left_words, 1)
-        for q in range(4):
-            load_scales(nc.sync, rs, right_scales, q)
         nc.vector.memset(ls[:].rearrange("p g n -> p (g n)").bitcast(I32), 0)
-        for q in range(4):
-            load_scales(nc.scalar, ls, left_scales, q)
+        make_identity(nc, ident[:])
         load_field(nc.sync, 0, field_a)
         load_field(nc.sync, 1, field_b)
+        load_words(nc.sync, lw, left_words, 0)
+        load_words(nc.sync, rw, right_words, 0)
+        for q in range(4):
+            load_scales(nc.scalar, ls, left_scales, q)
+        load_scales(nc.gpsimd, rs, right_scales, 0)
+        load_scales(nc.gpsimd, rs, right_scales, 1)
+        load_scales(nc.scalar, rs, right_scales, 2)
+        load_scales(nc.scalar, rs, right_scales, 3)
+        load_words(nc.sync, lw, left_words, 1)
         load_words(nc.sync, rw, right_words, 1)
-        make_identity(nc, ident[:])
-        nc.vector.memset(warm[:], 0.0)
-        nc.scalar.activation(out=warm[:], in_=warm[:], func=ACT.Copy)
         nc.vector.memset(wz[:], 0.0)
+        nc.vector.memset(warm[:], 0.0)
         nc.vector.memset(frow32[:], 0.0)
-        wb = bank()
-        for i in range(6):
-            nc.tensor.matmul(wb[:], wz[:, 0:P], wz[:], start=True, stop=True)
+        nc.scalar.activation(out=warm[:], in_=warm[:], func=ACT.Copy)
 
+        def keep_warm(n):
+            wb = misc_bank()
+            for i in range(n):
+                nc.tensor.matmul(wb[:], wz[:, 0:P], wz[:], start=True, stop=True)
+
+        keep_warm(4)
 
         def permute_scales(gc):
             for gk in range(G):
@@ -171,8 +176,8 @@ def tile_ising_transfer_fourth_power_s4_kernel(
 
         flipped = {}
 
-        def flip(r, g):
-            y = turn_bank()
+        def flip(r, g, early=False):
+            y = bank() if early else turn_bank()
             for t in range(T):
                 nc.tensor.transpose(y[:, t * P : (t + 1) * P], p_rows[r][:, g * H + t * P : g * H + (t + 1) * P], ident[:])
             flipped[r, g] = y
@@ -181,7 +186,12 @@ def tile_ising_transfer_fourth_power_s4_kernel(
             y = turn_bank()
             for t in range(T):
                 nc.tensor.transpose(y[:, t * P : (t + 1) * P], p_rows[4 + t][:, t2 * P : (t2 + 1) * P], ident[:])
-            nc.scalar.activation(out=a_raw[:, t2, :], in_=y[:], func=ACT.Copy, scale=fcol[:, t2 : t2 + 1])
+            flipped[t2] = y
+            if t2 < 3:
+                nc.scalar.activation(out=a_raw[:, t2, :], in_=y[:], func=ACT.Copy, scale=fcol[:, t2 : t2 + 1])
+
+        def carry(c0, c1):
+            nc.vector.tensor_scalar(out=a_raw[:, 3, c0:c1], in0=flipped[3][:, c0:c1], scalar1=fcol[:, 3:4], scalar2=None, op0=ALU.mult)
 
         def b_group(engine, g, h, n0=0, n=H):
             o = b_grp[g][h][:, n0 : n0 + n, :]
@@ -229,8 +239,8 @@ def tile_ising_transfer_fourth_power_s4_kernel(
 
         out_rows = out.rearrange("(g a t b) n -> g t a b n", g=G, a=A, t=T, b=B)
 
-        def product(r, h, engines="s"):
-            acc = bank()
+        def product(r, h, engines="s", spare=False):
+            acc = misc_bank() if spare else bank()
             for g in range(G):
                 nc.tensor.matmul_mx(
                     out=acc[:],
@@ -251,77 +261,83 @@ def tile_ising_transfer_fourth_power_s4_kernel(
                     nc.scalar.copy(out=res[:, cols], in_=acc[:, cols])
                 nc.sync.dma_start(out=out_rows[r // 4, r % 4][:, :, h * H + i * n : h * H + (i + 1) * n], in_=res[:, cols])
 
-        blocks = [(4 * gc + t, h) for h in range(2) for gc in range(G) for t in range(T)]
+        field_columns()
+        keep_warm(4)
         permute_scales(0)
         permute_words(0)
         permute_scales(1)
         permute_words(1)
+        blocks = [(4 * gc + t, h) for h in range(2) for gc in range(G) for t in range(T)]
         for k, (r, h) in enumerate(blocks):
             acc = first_product(r, h)
-            if k == 1:
-                field_columns()
             if k < 15:
                 hold(r, h, acc)
+                largest(r, h * H, h * H + H, rmax[:, D + k : D + k + 1])
             else:
                 hold(r, h, acc, 0, 2)
+                largest(r, H, H + 256, rmax[:, D + 15 : D + 16])
                 hold(r, h, acc, 2, 4)
-            if k >= 1:
-                j = k - 1
-                r2, h2 = blocks[j]
-                largest(r2, h2 * H, h2 * H + H, rmax[:, D + j : D + j + 1])
-                field_rows(r2, h2)
-        field_rows(7, 1)
-        largest(7, H, H + 256, rmax[:, D + 15 : D + 16])
+            field_rows(r, h)
         largest(7, H + 256, D + 16, rall[:])
         for t in range(T):
             flip_across(t)
-        flip(0, 0)
+            if t % 2:
+                keep_warm(1)
+        carry(0, 256)
         mb = misc_bank()
         nc.tensor.transpose(mb[:, 0:P], rall[:, 0:1].to_broadcast([P, P]), ident[:])
         nc.vector.tensor_reduce(out=mx[:], in_=mb[:, 0:P], axis=AX.X, op=ALU.max)
+        carry(256, 384)
         nc.vector.reciprocal(out=rm[:], in_=mx[:])
-        flip(0, 1)
-        flip(1, 0)
+        carry(384, 512)
+        flip(0, 0, True)
+        flip(0, 1, True)
+        keep_warm(1)
+        flip(1, 0, True)
         flip(1, 1)
-        b_group("s", 0, 0)
-        b_group("g", 1, 0, 0, 256)
-        b_group("g", 1, 0, 256, 256)
-        b_group("s", 0, 1)
-        b_group("s", 1, 1)
-        a_group(0, 0)
-        a_group(0, 1)
+        keep_warm(1)
         flip(2, 0)
         flip(2, 1)
+        flip(3, 0)
+        b_group("s", 0, 0)
+        b_group("s", 1, 0, 256, 256)
+        b_group("s", 0, 1)
+        b_group("s", 1, 1, 0, 256)
+        a_group(0, 0)
+        a_group(0, 1)
+        keep_warm(2)
         a_group(1, 0)
         a_group(1, 1)
-        flip(3, 0)
         flip(3, 1)
+        keep_warm(2)
+        b_group("v", 1, 0, 0, 256)
         b_quantize(0, 0)
         b_quantize(1, 0)
         a_quantize(0)
         a_quantize(1)
         product(0, 0)
         product(1, 0)
+        b_group("v", 1, 1, 256, 256)
         a_group(2, 0)
-        a_group(2, 1)
         flip(4, 1)
+        a_group(2, 1)
         flip(5, 1)
         b_quantize(0, 1)
         a_quantize(2)
         product(2, 0)
-        a_group(3, 0)
-        a_group(3, 1)
-        flip(6, 1)
-        flip(7, 1)
         b_quantize(1, 1)
         product(0, 1)
         product(1, 1)
         product(2, 1)
+        a_group(3, 0)
+        flip(6, 1)
+        a_group(3, 1)
+        flip(7, 1)
+        a_group(4, 0)
         a_quantize(3)
+        a_group(4, 1)
         product(3, 0)
         product(3, 1)
-        a_group(4, 0)
-        a_group(4, 1)
         for r in range(5, 8):
             a_group(r, 0)
             a_quantize(r - 1)

@@ -66,14 +66,14 @@ def tile_ising_transfer_fourth_power_s4_kernel(
         rall = keep.tile([P, 1], F32, name="rall")
         mx = keep.tile([P, 1], F32, name="mx")
         rm = keep.tile([P, 1], F32, name="rm")
-        p_rows = [keep.tile([P, D + 16], F32, name="p_rows%d" % r, align_bytes=256) for r in range(8)]
+        p_rows = [keep.tile([P, T, D + 16], F32, name="p_rows%d" % g, align_bytes=256) for g in range(G)]
         b_rows = [keep.tile([P, T, D], F32, name="b_rows%d" % g, align_bytes=256) for g in range(G)]
         b_codes = [[keep.tile([P, H], U32, name="b_codes%d%d" % (g, h), align_bytes=256) for h in range(2)] for g in range(G)]
         b_scales = [[keep.tile([P, H], U8, name="b_scales%d%d" % (g, h), align_bytes=256) for h in range(2)] for g in range(G)]
         b_grp = [[keep.tile([P, H, T], BF16, name="b_grp%d%d" % (g, h), align_bytes=256) for h in range(2)] for g in range(G)]
         a_codes = [keep.tile([P, G * P], U32, name="a_codes%d" % r, align_bytes=256) for r in range(8)]
         a_scales = [keep.tile([P, G * P], U8, name="a_scales%d" % r, align_bytes=256) for r in range(8)]
-        rmax = p_rows[7]
+        rmax = p_rows[1][:, 3, :]
 
         def load_words(engine, dst, src, half):
             cols = slice(half * D, (half + 1) * D)
@@ -115,7 +115,7 @@ def tile_ising_transfer_fourth_power_s4_kernel(
             for i in range(n):
                 nc.tensor.matmul(wb[:], wz[:, 0:P], wz[:], start=True, stop=True)
 
-        keep_warm(4)
+        keep_warm(3)
 
         def permute_scales(gc):
             for gk in range(G):
@@ -138,8 +138,8 @@ def tile_ising_transfer_fourth_power_s4_kernel(
                 nc.tensor.transpose(fb[:, g * P : (g + 1) * P], frow32[:, g * P : (g + 1) * P], ident[:])
             nc.vector.tensor_copy(out=fcol[:].rearrange("p (g x) -> p g x", g=G), in_=fb[:, 0 : 2 * P].rearrange("p (g x) -> p g x", g=G)[:, :, 0:8])
 
-        def first_product(r, h):
-            acc = bank()
+        def first_product(r, h, odd):
+            acc = turn_bank() if odd else bank()
             for gk in range(G):
                 nc.tensor.matmul_mx(
                     out=acc[:],
@@ -153,21 +153,21 @@ def tile_ising_transfer_fourth_power_s4_kernel(
             return acc
 
         def half_rows(r, h):
-            return p_rows[r][:, h * H : (h + 1) * H]
+            return p_rows[r // T][:, r % T, h * H : (h + 1) * H]
 
         def hold(r, h, acc, t0=0, t1=T):
             nc.scalar.copy(
-                out=p_rows[r][:, h * H + t0 * P : h * H + t1 * P].rearrange("p (t a b) -> p t a b", t=t1 - t0, a=A),
+                out=p_rows[r // T][:, r % T, h * H + t0 * P : h * H + t1 * P].rearrange("p (t a b) -> p t a b", t=t1 - t0, a=A),
                 in_=acc[:].rearrange("p (a t b) -> p t a b", t=T, a=A)[:, t0:t1],
             )
 
         def largest(r, c0, c1, out):
-            nc.vector.tensor_reduce(out=out, in_=p_rows[r][:, c0:c1], axis=AX.X, op=ALU.max, apply_absolute_value=True)
+            nc.vector.tensor_reduce(out=out, in_=p_rows[r // T][:, r % T, c0:c1], axis=AX.X, op=ALU.max, apply_absolute_value=True)
 
         def field_rows(r, h):
             nc.gpsimd.tensor_scalar(
-                out=b_rows[r // 4][:, r % 4, h * H : (h + 1) * H].rearrange("p (a t b) -> p a t b", t=T, a=A),
-                in0=half_rows(r, h).rearrange("p (t a b) -> p a t b", t=T, a=A),
+                out=b_rows[r // T][:, r % T, h * H : (h + 1) * H],
+                in0=half_rows(r, h),
                 scalar1=fcol[:, 8 * (r // 4) + 4 + r % 4 : 8 * (r // 4) + 5 + r % 4],
                 scalar2=0.0,
                 op0=ALU.mult,
@@ -179,13 +179,13 @@ def tile_ising_transfer_fourth_power_s4_kernel(
         def flip(r, g, early=False):
             y = bank() if early else turn_bank()
             for t in range(T):
-                nc.tensor.transpose(y[:, t * P : (t + 1) * P], p_rows[r][:, g * H + t * P : g * H + (t + 1) * P], ident[:])
+                nc.tensor.transpose(y[:, t * P : (t + 1) * P], p_rows[r // T][:, r % T, g * H + t * P : g * H + (t + 1) * P], ident[:])
             flipped[r, g] = y
 
         def flip_across(t2):
             y = turn_bank()
             for t in range(T):
-                nc.tensor.transpose(y[:, t * P : (t + 1) * P], p_rows[4 + t][:, t2 * P : (t2 + 1) * P], ident[:])
+                nc.tensor.transpose(y[:, t * P : (t + 1) * P], p_rows[1][:, t, t2 * P : (t2 + 1) * P], ident[:])
             flipped[t2] = y
             if t2 < 3:
                 nc.scalar.activation(out=a_raw[:, t2, :], in_=y[:], func=ACT.Copy, scale=fcol[:, t2 : t2 + 1])
@@ -194,9 +194,18 @@ def tile_ising_transfer_fourth_power_s4_kernel(
             nc.vector.tensor_scalar(out=a_raw[:, 3, c0:c1], in0=flipped[3][:, c0:c1], scalar1=fcol[:, 3:4], scalar2=None, op0=ALU.mult)
 
         def b_group(engine, g, h, n0=0, n=H):
-            o = b_grp[g][h][:, n0 : n0 + n, :]
-            i = b_rows[g][:, :, h * H + n0 : h * H + n0 + n].rearrange("p t n -> p n t")
-            if engine == "s":
+            o = b_grp[g][h][:, n0 : n0 + n, :].rearrange("p (c i) t -> p c t i", i=4)
+            i = b_rows[g][:, :, h * H + n0 : h * H + n0 + n].rearrange("p t (c i) -> p c t i", i=4)
+            if engine == "f":
+                nc.vector.scalar_tensor_tensor(
+                    out=b_grp[g][h][:, n0 : n0 + n, :],
+                    in0=p_rows[g][:, :, h * H + n0 : h * H + n0 + n].rearrange("p t n -> p n t"),
+                    scalar=rm[:, 0:1],
+                    in1=fcol[:, 8 * g + 4 : 8 * g + 8].unsqueeze(1).to_broadcast([P, n, T]),
+                    op0=ALU.mult,
+                    op1=ALU.mult,
+                )
+            elif engine == "s":
                 nc.scalar.activation(out=o, in_=i, func=ACT.Copy, scale=rm[:, 0:1])
             elif engine == "v":
                 nc.vector.tensor_scalar(out=o, in0=i, scalar1=rm[:, 0:1], scalar2=None, op0=ALU.mult)
@@ -218,8 +227,8 @@ def tile_ising_transfer_fourth_power_s4_kernel(
                 a_grp[r] = tile_a
             if r >= 4 and g == 0:
                 nc.vector.tensor_scalar(
-                    out=a_grp[r][:, g, :, :],
-                    in0=a_raw[:, :, (r - 4) * P : (r - 3) * P].rearrange("p t n -> p n t"),
+                    out=a_grp[r][:, g, :, :].rearrange("p (c i) t -> p c t i", i=4),
+                    in0=a_raw[:, :, (r - 4) * P : (r - 3) * P].rearrange("p t (c i) -> p c t i", i=4),
                     scalar1=rm[:, 0:1],
                     scalar2=None,
                     op0=ALU.mult,
@@ -255,21 +264,28 @@ def tile_ising_transfer_fourth_power_s4_kernel(
             n = H // len(engines)
             for i, e in enumerate(engines):
                 cols = slice(i * n, (i + 1) * n)
+                blocks_i = slice(i * A // len(engines), (i + 1) * A // len(engines))
+                o = res[:, cols].rearrange("p (a t b) -> p a t b", t=T, b=B)
+                s = acc[:].rearrange("p (t a b) -> p a t b", t=T, a=A)[:, blocks_i]
                 if e == "v":
-                    nc.vector.tensor_copy(out=res[:, cols], in_=acc[:, cols])
+                    nc.vector.tensor_copy(out=o, in_=s)
                 else:
-                    nc.scalar.copy(out=res[:, cols], in_=acc[:, cols])
+                    nc.scalar.copy(out=o, in_=s)
                 nc.sync.dma_start(out=out_rows[r // 4, r % 4][:, :, h * H + i * n : h * H + (i + 1) * n], in_=res[:, cols])
 
-        field_columns()
-        keep_warm(4)
+        nc.vector.tensor_copy(out=frow32[0:8, :], in_=frow[0:8, :])
+        fb = bank()
+        for g in range(G):
+            nc.tensor.transpose(fb[:, g * P : (g + 1) * P], frow32[:, g * P : (g + 1) * P], ident[:])
+        keep_warm(3)
         permute_scales(0)
         permute_words(0)
         permute_scales(1)
+        nc.vector.tensor_copy(out=fcol[:].rearrange("p (g x) -> p g x", g=G), in_=fb[:, 0 : 2 * P].rearrange("p (g x) -> p g x", g=G)[:, :, 0:8])
         permute_words(1)
         blocks = [(4 * gc + t, h) for h in range(2) for gc in range(G) for t in range(T)]
         for k, (r, h) in enumerate(blocks):
-            acc = first_product(r, h)
+            acc = first_product(r, h, k % 2)
             if k < 15:
                 hold(r, h, acc)
                 largest(r, h * H, h * H + H, rmax[:, D + k : D + k + 1])
@@ -302,7 +318,7 @@ def tile_ising_transfer_fourth_power_s4_kernel(
         b_group("s", 0, 0)
         b_group("s", 1, 0, 256, 256)
         b_group("s", 0, 1)
-        b_group("s", 1, 1, 0, 256)
+        b_group("s", 1, 1)
         a_group(0, 0)
         a_group(0, 1)
         keep_warm(2)
@@ -317,20 +333,19 @@ def tile_ising_transfer_fourth_power_s4_kernel(
         a_quantize(1)
         product(0, 0)
         product(1, 0)
-        b_group("v", 1, 1, 256, 256)
         a_group(2, 0)
         flip(4, 1)
         a_group(2, 1)
         flip(5, 1)
-        b_quantize(0, 1)
         a_quantize(2)
         product(2, 0)
+        b_quantize(0, 1)
+        a_group(3, 0)
+        flip(6, 1)
         b_quantize(1, 1)
         product(0, 1)
         product(1, 1)
         product(2, 1)
-        a_group(3, 0)
-        flip(6, 1)
         a_group(3, 1)
         flip(7, 1)
         a_group(4, 0)

from contextlib import ExitStack

import concourse.mybir as mybir
from concourse.masks import make_identity

F32 = mybir.dt.float32
BF16 = mybir.dt.bfloat16
I32 = mybir.dt.int32
U32 = mybir.dt.uint32
U8 = mybir.dt.uint8
FP8X4 = mybir.dt.float8_e4m3fn_x4
FP4X4 = mybir.dt.float4_e2m1fn_x4
ALU = mybir.AluOpType
AX = mybir.AxisListType
ACT = mybir.ActivationFunctionType

D = 1024
P = 128
G = 2
T = 4
A = 16
B = 8
H = 512

FLOPS = 2 * 2 * D * D * D


def tile_ising_transfer_fourth_power_s4_kernel(
    tc, left_words, left_scales, right_words, right_scales, field_a, field_b, out
):
    nc = tc.nc
    with ExitStack() as ctx:
        keep = ctx.enter_context(tc.tile_pool(name="keep", bufs=1))
        stage = ctx.enter_context(tc.tile_pool(name="stage", bufs=8))
        results = ctx.enter_context(tc.tile_pool(name="results", bufs=16))
        psum = ctx.enter_context(tc.psum_pool(name="psum", bufs=3))
        turn = ctx.enter_context(tc.psum_pool(name="turn", bufs=4))
        misc = ctx.enter_context(tc.psum_pool(name="misc", bufs=1))
        ctx.enter_context(tc.manual_schedule())

        def bank():
            b = psum.tile([P, H], F32, name="bank")
            return b

        def turn_bank():
            tb = turn.tile([P, H], F32, name="tbank")
            return tb

        def misc_bank():
            mb = misc.tile([P, H], F32, name="mbank")
            return mb

        lw = keep.tile([P, G, 2 * D], U8, name="lw", align_bytes=256)
        rw = keep.tile([P, G, 2 * D], U8, name="rw", align_bytes=256)
        ls = keep.tile([P, G, D], U8, name="ls", align_bytes=256)
        rs = keep.tile([P, G, D], U8, name="rs", align_bytes=256)
        lwp = keep.tile([P, G, 8, 2 * P], U8, name="lwp", align_bytes=256)
        lsp = keep.tile([P, G, 8, P], U8, name="lsp", align_bytes=256)
        frow = keep.tile([P, 2 * P], BF16, name="frow", align_bytes=256)
        frow32 = keep.tile([P, 2 * P], F32, name="frow32", align_bytes=256)
        fcol = keep.tile([P, 16], F32, name="fcol", align_bytes=256)
        ident = keep.tile([P, P], F32, name="ident", align_bytes=256)
        warm = keep.tile([P, 1], F32, name="warm")
        wz = keep.tile([P, H], BF16, name="wz", align_bytes=256)
        a_raw = keep.tile([P, T, H], F32, name="a_raw", align_bytes=256)
        rall = keep.tile([P, 1], F32, name="rall")
        mx = keep.tile([P, 1], F32, name="mx")
        rm = keep.tile([P, 1], F32, name="rm")
        p_rows = [keep.tile([P, T, D + 16], F32, name="p_rows%d" % g, align_bytes=256) for g in range(G)]
        b_rows = [keep.tile([P, T, D], F32, name="b_rows%d" % g, align_bytes=256) for g in range(G)]
        b_codes = [[keep.tile([P, H], U32, name="b_codes%d%d" % (g, h), align_bytes=256) for h in range(2)] for g in range(G)]
        b_scales = [[keep.tile([P, H], U8, name="b_scales%d%d" % (g, h), align_bytes=256) for h in range(2)] for g in range(G)]
        b_grp = [[keep.tile([P, H, T], BF16, name="b_grp%d%d" % (g, h), align_bytes=256) for h in range(2)] for g in range(G)]
        a_codes = [keep.tile([P, G * P], U32, name="a_codes%d" % r, align_bytes=256) for r in range(8)]
        a_scales = [keep.tile([P, G * P], U8, name="a_scales%d" % r, align_bytes=256) for r in range(8)]
        rmax = p_rows[1][:, 3, :]

        def load_words(engine, dst, src, half):
            cols = slice(half * D, (half + 1) * D)
            engine.dma_start(out=dst[:, :, cols].bitcast(I32), in_=src[:, :, cols].rearrange("g p n -> p g n").bitcast(I32))

        def load_scales(engine, dst, src, q):
            engine.dma_start(
                out=dst[32 * q : 32 * q + 4, :, :].bitcast(I32),
                in_=src[:, 4 * q : 4 * q + 4, :].rearrange("g q n -> q g n").bitcast(I32),
            )

        def load_field(engine, i, f):
            engine.dma_start(
                out=frow[4 * i : 4 * i + 4, :].rearrange("t (c b) -> t c b", b=B),
                in_=f.rearrange("(c t b) -> t c b", t=T, b=B),
            )

        nc.vector.memset(ls[:].rearrange("p g n -> p (g n)").bitcast(I32), 0)
        make_identity(nc, ident[:])
        load_field(nc.sync, 0, field_a)
        load_field(nc.sync, 1, field_b)
        load_words(nc.sync, lw, left_words, 0)
        load_words(nc.sync, rw, right_words, 0)
        for q in range(4):
            load_scales(nc.scalar, ls, left_scales, q)
        load_scales(nc.gpsimd, rs, right_scales, 0)
        load_scales(nc.gpsimd, rs, right_scales, 1)
        load_scales(nc.scalar, rs, right_scales, 2)
        load_scales(nc.scalar, rs, right_scales, 3)
        load_words(nc.sync, lw, left_words, 1)
        load_words(nc.sync, rw, right_words, 1)
        nc.vector.memset(wz[:], 0.0)
        nc.vector.memset(warm[:], 0.0)
        nc.vector.memset(frow32[:], 0.0)
        nc.scalar.activation(out=warm[:], in_=warm[:], func=ACT.Copy)

        def keep_warm(n):
            wb = misc_bank()
            for i in range(n):
                nc.tensor.matmul(wb[:], wz[:, 0:P], wz[:], start=True, stop=True)

        keep_warm(3)

        def permute_scales(gc):
            for gk in range(G):
                nc.vector.tensor_copy(
                    out=lsp[:, gk, 4 * gc : 4 * gc + 4, :].rearrange("p r n -> p (r n)").bitcast(I32).rearrange("p (t a b) -> p t a b", t=T, a=A),
                    in_=ls[:, gk, gc * H : (gc + 1) * H].bitcast(I32).rearrange("p (a t b) -> p t a b", t=T, a=A),
                )

        def permute_words(gc):
            for gk in range(G):
                nc.vector.tensor_copy(
                    out=lwp[:, gk, 4 * gc : 4 * gc + 4, :].rearrange("p r n -> p (r n)").bitcast(I32).rearrange("p (t a b) -> p t a b", t=T, a=A),
                    in_=lw[:, gk, gc * D : (gc + 1) * D].bitcast(I32).rearrange("p (a t b) -> p t a b", t=T, a=A),
                )

        def field_columns():
            nc.vector.tensor_copy(out=frow32[0:8, :], in_=frow[0:8, :])
            fb = misc_bank()
            for g in range(G):
                nc.tensor.transpose(fb[:, g * P : (g + 1) * P], frow32[:, g * P : (g + 1) * P], ident[:])
            nc.vector.tensor_copy(out=fcol[:].rearrange("p (g x) -> p g x", g=G), in_=fb[:, 0 : 2 * P].rearrange("p (g x) -> p g x", g=G)[:, :, 0:8])

        def first_product(r, h, odd):
            acc = turn_bank() if odd else bank()
            for gk in range(G):
                nc.tensor.matmul_mx(
                    out=acc[:],
                    lhsT=lwp[:, gk, r, :].bitcast(FP4X4),
                    lhsT_scale=lsp[:, gk, r, :],
                    rhs=rw[:, gk, h * D : (h + 1) * D].bitcast(FP4X4),
                    rhs_scale=rs[:, gk, h * H : (h + 1) * H],
                    start=(gk == 0),
                    stop=(gk == 1),
                )
            return acc

        def half_rows(r, h):
            return p_rows[r // T][:, r % T, h * H : (h + 1) * H]

        def hold(r, h, acc, t0=0, t1=T):
            nc.scalar.copy(
                out=p_rows[r // T][:, r % T, h * H + t0 * P : h * H + t1 * P].rearrange("p (t a b) -> p t a b", t=t1 - t0, a=A),
                in_=acc[:].rearrange("p (a t b) -> p t a b", t=T, a=A)[:, t0:t1],
            )

        def largest(r, c0, c1, out):
            nc.vector.tensor_reduce(out=out, in_=p_rows[r // T][:, r % T, c0:c1], axis=AX.X, op=ALU.max, apply_absolute_value=True)

        def field_rows(r, h):
            nc.gpsimd.tensor_scalar(
                out=b_rows[r // T][:, r % T, h * H : (h + 1) * H],
                in0=half_rows(r, h),
                scalar1=fcol[:, 8 * (r // 4) + 4 + r % 4 : 8 * (r // 4) + 5 + r % 4],
                scalar2=0.0,
                op0=ALU.mult,
                op1=ALU.add,
            )

        flipped = {}

        def flip(r, g, early=False):
            y = bank() if early else turn_bank()
            for t in range(T):
                nc.tensor.transpose(y[:, t * P : (t + 1) * P], p_rows[r // T][:, r % T, g * H + t * P : g * H + (t + 1) * P], ident[:])
            flipped[r, g] = y

        def flip_across(t2):
            y = turn_bank()
            for t in range(T):
                nc.tensor.transpose(y[:, t * P : (t + 1) * P], p_rows[1][:, t, t2 * P : (t2 + 1) * P], ident[:])
            flipped[t2] = y
            if t2 < 3:
                nc.scalar.activation(out=a_raw[:, t2, :], in_=y[:], func=ACT.Copy, scale=fcol[:, t2 : t2 + 1])

        def carry(c0, c1):
            nc.vector.tensor_scalar(out=a_raw[:, 3, c0:c1], in0=flipped[3][:, c0:c1], scalar1=fcol[:, 3:4], scalar2=None, op0=ALU.mult)

        def b_group(engine, g, h, n0=0, n=H):
            o = b_grp[g][h][:, n0 : n0 + n, :].rearrange("p (c i) t -> p c t i", i=4)
            i = b_rows[g][:, :, h * H + n0 : h * H + n0 + n].rearrange("p t (c i) -> p c t i", i=4)
            if engine == "f":
                nc.vector.scalar_tensor_tensor(
                    out=b_grp[g][h][:, n0 : n0 + n, :],
                    in0=p_rows[g][:, :, h * H + n0 : h * H + n0 + n].rearrange("p t n -> p n t"),
                    scalar=rm[:, 0:1],
                    in1=fcol[:, 8 * g + 4 : 8 * g + 8].unsqueeze(1).to_broadcast([P, n, T]),
                    op0=ALU.mult,
                    op1=ALU.mult,
                )
            elif engine == "s":
                nc.scalar.activation(out=o, in_=i, func=ACT.Copy, scale=rm[:, 0:1])
            elif engine == "v":
                nc.vector.tensor_scalar(out=o, in0=i, scalar1=rm[:, 0:1], scalar2=None, op0=ALU.mult)
            else:
                nc.gpsimd.tensor_scalar(out=o, in0=i, scalar1=rm[:, 0:1], scalar2=0.0, op0=ALU.mult, op1=ALU.add)

        def b_quantize(g, h, n0=0, n=H):
            nc.vector.quantize_mx(
                out=b_codes[g][h][:, n0 : n0 + n].bitcast(FP8X4),
                scales=b_scales[g][h][:, n0 : n0 + n],
                in_=b_grp[g][h][:, n0 : n0 + n, :].rearrange("p n t -> p (n t)"),
            )

        a_grp = {}

        def a_group(r, g):
            if r not in a_grp:
                tile_a = stage.tile([P, G, P, T], BF16, name="a_grp", align_bytes=256)
                a_grp[r] = tile_a
            if r >= 4 and g == 0:
                nc.vector.tensor_scalar(
                    out=a_grp[r][:, g, :, :].rearrange("p (c i) t -> p c t i", i=4),
                    in0=a_raw[:, :, (r - 4) * P : (r - 3) * P].rearrange("p t (c i) -> p c t i", i=4),
                    scalar1=rm[:, 0:1],
                    scalar2=None,
                    op0=ALU.mult,
                )
                return
            nc.vector.scalar_tensor_tensor(
                out=a_grp[r][:, g, :, :],
                in0=flipped[r, g][:].rearrange("p (t n) -> p n t", t=T),
                scalar=rm[:, 0:1],
                in1=fcol[:, 8 * g : 8 * g + 4].unsqueeze(1).to_broadcast([P, P, T]),
                op0=ALU.mult,
                op1=ALU.mult,
            )

        def a_quantize(r):
            nc.vector.quantize_mx(out=a_codes[r][:].bitcast(FP8X4), scales=a_scales[r][:], in_=a_grp[r][:].rearrange("p g n t -> p (g n t)"))

        out_rows = out.rearrange("(g a t b) n -> g t a b n", g=G, a=A, t=T, b=B)

        def product(r, h, engines="s", spare=False):
            acc = misc_bank() if spare else bank()
            for g in range(G):
                nc.tensor.matmul_mx(
                    out=acc[:],
                    lhsT=a_codes[r][:, g * P : (g + 1) * P].bitcast(FP8X4),
                    lhsT_scale=a_scales[r][:, g * P : (g + 1) * P],
                    rhs=b_codes[g][h][:].bitcast(FP8X4),
                    rhs_scale=b_scales[g][h][:],
                    start=(g == 0),
                    stop=(g == 1),
                )
            res = results.tile([P, H], F32, name="res", align_bytes=256)
            n = H // len(engines)
            for i, e in enumerate(engines):
                cols = slice(i * n, (i + 1) * n)
                blocks_i = slice(i * A // len(engines), (i + 1) * A // len(engines))
                o = res[:, cols].rearrange("p (a t b) -> p a t b", t=T, b=B)
                s = acc[:].rearrange("p (t a b) -> p a t b", t=T, a=A)[:, blocks_i]
                if e == "v":
                    nc.vector.tensor_copy(out=o, in_=s)
                else:
                    nc.scalar.copy(out=o, in_=s)
                nc.sync.dma_start(out=out_rows[r // 4, r % 4][:, :, h * H + i * n : h * H + (i + 1) * n], in_=res[:, cols])

        nc.vector.tensor_copy(out=frow32[0:8, :], in_=frow[0:8, :])
        fb = bank()
        for g in range(G):
            nc.tensor.transpose(fb[:, g * P : (g + 1) * P], frow32[:, g * P : (g + 1) * P], ident[:])
        keep_warm(3)
        permute_scales(0)
        permute_words(0)
        permute_scales(1)
        nc.vector.tensor_copy(out=fcol[:].rearrange("p (g x) -> p g x", g=G), in_=fb[:, 0 : 2 * P].rearrange("p (g x) -> p g x", g=G)[:, :, 0:8])
        permute_words(1)
        blocks = [(4 * gc + t, h) for h in range(2) for gc in range(G) for t in range(T)]
        for k, (r, h) in enumerate(blocks):
            acc = first_product(r, h, k % 2)
            if k < 15:
                hold(r, h, acc)
                largest(r, h * H, h * H + H, rmax[:, D + k : D + k + 1])
            else:
                hold(r, h, acc, 0, 2)
                largest(r, H, H + 256, rmax[:, D + 15 : D + 16])
                hold(r, h, acc, 2, 4)
            field_rows(r, h)
        largest(7, H + 256, D + 16, rall[:])
        for t in range(T):
            flip_across(t)
            if t % 2:
                keep_warm(1)
        carry(0, 256)
        mb = misc_bank()
        nc.tensor.transpose(mb[:, 0:P], rall[:, 0:1].to_broadcast([P, P]), ident[:])
        nc.vector.tensor_reduce(out=mx[:], in_=mb[:, 0:P], axis=AX.X, op=ALU.max)
        carry(256, 384)
        nc.vector.reciprocal(out=rm[:], in_=mx[:])
        carry(384, 512)
        flip(0, 0, True)
        flip(0, 1, True)
        keep_warm(1)
        flip(1, 0, True)
        flip(1, 1)
        keep_warm(1)
        flip(2, 0)
        flip(2, 1)
        flip(3, 0)
        b_group("s", 0, 0)
        b_group("s", 1, 0, 256, 256)
        b_group("s", 0, 1)
        b_group("s", 1, 1)
        a_group(0, 0)
        a_group(0, 1)
        keep_warm(2)
        a_group(1, 0)
        a_group(1, 1)
        flip(3, 1)
        keep_warm(2)
        b_group("v", 1, 0, 0, 256)
        b_quantize(0, 0)
        b_quantize(1, 0)
        a_quantize(0)
        a_quantize(1)
        product(0, 0)
        product(1, 0)
        a_group(2, 0)
        flip(4, 1)
        a_group(2, 1)
        flip(5, 1)
        a_quantize(2)
        product(2, 0)
        b_quantize(0, 1)
        a_group(3, 0)
        flip(6, 1)
        b_quantize(1, 1)
        product(0, 1)
        product(1, 1)
        product(2, 1)
        a_group(3, 1)
        flip(7, 1)
        a_group(4, 0)
        a_quantize(3)
        a_group(4, 1)
        product(3, 0)
        product(3, 1)
        for r in range(5, 8):
            a_group(r, 0)
            a_quantize(r - 1)
            a_group(r, 1)
            product(r - 1, 0)
            product(r - 1, 1)
        a_quantize(7)
        product(7, 0, "v")
        product(7, 1, "vs")
